import numpy as np
import ml_dtypes


def mxq(x, axis, fmt="e4m3"):
    dtype, down = {"e4m3": (ml_dtypes.float8_e4m3fn, 7), "e5m2": (ml_dtypes.float8_e5m2, 14)}[fmt]
    v = np.moveaxis(np.asarray(x, np.float32).astype(ml_dtypes.bfloat16).astype(np.float64), axis, -1)
    blocks = v.reshape(v.shape[:-1] + (-1, 32))
    amax = np.abs(blocks).max(-1, keepdims=True)
    byte = np.maximum(np.where(amax > 0, np.frexp(amax)[1] - 1 + 127, 0) - down, 1)
    scale = np.exp2(byte - 127.0)
    codes = (blocks / scale).astype(np.float32).astype(dtype).astype(np.float64)
    return np.moveaxis((codes * scale).reshape(v.shape), -1, axis)


WIDE = False


def mx_kscale(k):
    if not WIDE:
        return np.ones(k)
    levels = np.array([10, -10, 5, -5, 0])
    if k % 512:
        return np.exp2(np.random.permutation(np.resize(levels, k // 32))).repeat(32)
    a = np.empty((k // 512, 16))
    for p in range(k // 512):
        a[p, :8] = np.random.permutation(np.resize(levels, 8))
        for g in range(8):
            far = levels[np.abs(levels - a[p, g]) >= 10]
            a[p, g + 8] = far[np.random.randint(len(far))]
    return np.exp2(a.ravel()).repeat(32)


BF16 = ml_dtypes.bfloat16


def bf(x):
    return np.asarray(x, np.float32).astype(BF16)


def f64(x):
    return np.asarray(x).astype(np.float64)


E2M1 = np.array([0.0, 0.5, 1.0, 1.5, 2.0, 3.0, 4.0, 6.0, -0.0, -0.5, -1.0, -1.5, -2.0, -3.0, -4.0, -6.0])


def pack_weight(w, fmt):
    k, n = w.shape
    w = f64(bf(w)).reshape(k // 32, 32, n)
    amax = np.abs(w).max(1)
    if fmt == "e4m3":
        byte = np.frexp(amax)[1] - 1 + 127 - 7
    else:
        mant, ex = np.frexp(amax / 6.0)
        byte = np.where(mant > 0.5, ex, ex - 1) + 127
    byte = np.clip(np.where(amax > 0, byte, 1), 1, 254)
    scaled = (w * np.exp2(127.0 - byte)[:, None, :]).reshape(k, n).astype(np.float32)
    by_word = np.ascontiguousarray(scaled.reshape(k // 512, 128, 4, n).transpose(0, 1, 3, 2))
    if fmt == "e4m3":
        words = by_word.astype(ml_dtypes.float8_e4m3fn).view(np.uint8)
    else:
        c = by_word.astype(ml_dtypes.float4_e2m1fn).view(np.uint8) & 0xF
        words = c[..., 0::2] | (c[..., 1::2] << 4)
    return np.ascontiguousarray(words), np.ascontiguousarray(byte.astype(np.uint8).reshape(k // 512, 16, n))


def unpack_weight(words, scales, fmt):
    g, p, n, _ = words.shape
    if fmt == "e4m3":
        vals = np.ascontiguousarray(words).view(ml_dtypes.float8_e4m3fn).astype(np.float64)
    else:
        nib = np.empty((g, p, n, 4), np.uint8)
        nib[..., 0::2] = words & 0xF
        nib[..., 1::2] = words >> 4
        vals = E2M1[nib]
    vals = vals * np.repeat(np.exp2(scales.astype(np.float64) - 127.0), 8, axis=1)[..., None]
    return vals.transpose(0, 1, 3, 2).reshape(g * 512, n)
def pack4(w):
    words, scales = pack_weight(w, "e2m1")
    return words.reshape(words.shape[0], 128, -1), scales


def unpack4(words, scales):
    return unpack_weight(words.reshape(words.shape[0], 128, -1, 2), scales, "e2m1")


def planes(Y):
    n, m = Y.shape
    b = f64(bf(Y)).reshape(n // 32, 32, m)
    amax = np.abs(b).max(1)
    byte = np.clip(np.where(amax > 0, np.frexp(amax)[1] - 1 + 127 - 7, 1), 1, 254)
    codes = (b * np.exp2(127.0 - byte)[:, None, :]).reshape(n, m).astype(np.float32).astype(ml_dtypes.float8_e4m3fn).view(np.uint8)
    words = codes.reshape(n // 512, 128, 4, m).transpose(0, 1, 3, 2)
    return np.ascontiguousarray(words), np.ascontiguousarray(byte.astype(np.uint8).reshape(n // 512, 16, m))


B, S, R, D, G = 2, 512, 4, 512, 16
C = D // G
K = 2 * R + R * R
RD = R * D
M = G * K
ROUNDS = 2


def sigmoid(v):
    return 1.0 / (1.0 + np.exp(-v))


def balance(l):
    q = np.exp(l)
    for _ in range(ROUNDS):
        q = q / np.sum(q, axis=-1, keepdims=True)
        q = q / np.sum(q, axis=-2, keepdims=True)
    return q


def read_streams(pre, xg):
    u = pre[..., 0][..., None] * xg[:, :, 0]
    for r in range(1, xg.shape[2]):
        u = u + pre[..., r][..., None] * xg[:, :, r]
    return u


def mix_streams(q, xg):
    qi = np.transpose(q, (0, 1, 3, 2, 4))
    y = qi[..., 0][..., None] * xg[:, :, 0][:, :, None]
    for j in range(1, xg.shape[2]):
        y = y + qi[..., j][..., None] * xg[:, :, j][:, :, None]
    return y


def setup_inputs():
    s, t = mx_kscale(RD), mx_kscale(D)
    x = bf(np.random.standard_normal((B, S, R, D)))
    gn = bf((1.0 + 0.1 * np.random.standard_normal(RD)) * s)
    phi_words, phi_scales = pack4(1.5 * np.random.standard_normal((RD, M)) / np.sqrt(RD) / s[:, None])
    bm = bf(0.5 * np.random.standard_normal(M))
    gf = bf((1.0 + 0.1 * np.random.standard_normal(D)) * t)
    w_words, w_scales = pack4(np.random.standard_normal((D, D)) / np.sqrt(D) / t[:, None])
    return {
        "x": x,
        "gn": gn,
        "phi_words": phi_words,
        "phi_scales": phi_scales,
        "bm": bm,
        "gf": gf,
        "w_words": w_words,
        "w_scales": w_scales,
    }


def core(x, gn, phi_words, phi_scales, bm, gf, w_words, w_scales):
    x = f64(x)
    b, s, r, d = x.shape

    xf = x.reshape(b, s, r * d)
    xn = xf * f64(gn)

    t = (mxq(xn, 2, "e4m3") @ unpack4(phi_words, phi_scales)) + f64(bm)
    t = t.reshape(b, s, G, K)

    pre = sigmoid(t[..., 0:r])
    post = 2.0 * sigmoid(t[..., r:2 * r])
    l = t[..., 2 * r:].reshape(b, s, G, r, r)

    q = balance(l)

    xg = x.reshape(b, s, r, G, C)
    u = read_streams(pre, xg).reshape(b, s, d)

    ug = u * f64(gf)

    h = np.maximum(mxq(ug, 2, "e4m3") @ unpack4(w_words, w_scales), 0.0)
    f = h * h
    fg = f.reshape(b, s, G, C)

    mixed = mix_streams(q, xg)
    post_i = np.transpose(post, (0, 1, 3, 2))
    y = mixed + post_i[..., None] * fg[:, :, None]
    return y.reshape(b, s, r, d)


def reference(x, gn, phi_words, phi_scales, bm, gf, w_words, w_scales):
    R_out = core(x, gn, phi_words, phi_scales, bm, gf, w_words, w_scales)
    words, scales = planes(np.moveaxis(R_out, 3, 0).reshape(512, -1))
    return R_out, words, scales

from contextlib import ExitStack

import concourse.mybir as mybir
from concourse.masks import make_identity

F32 = mybir.dt.float32
BF16 = mybir.dt.bfloat16
U32 = mybir.dt.uint32
I32 = mybir.dt.int32
U8 = mybir.dt.uint8
FP8X4 = mybir.dt.float8_e4m3fn_x4
FP4X4 = mybir.dt.float4_e2m1fn_x4
ACT = mybir.ActivationFunctionType
ALU = mybir.AluOpType
AX = mybir.AxisListType

P = 128
TOKENS = 1024
R = 4
D = 512
G = 16
K = 24
M = G * K
NT = TOKENS // P

FLOPS = 2 * TOKENS * (R * D) * M + 2 * TOKENS * D * D


def bc(ap, axis, n):
    a = ap.unsqueeze(axis)
    shape = list(a.shape)
    shape[axis] = n
    return a.to_broadcast(shape)


def tile_groupedmanifoldhyperconnection_x2_kernel(
    tc, x, gn, phi_words, phi_scales, bm, gf, w_words, w_scales, out_0, out_1, out_2
):
    nc = tc.nc
    x_rows = x.rearrange("b s r d -> (b s) (r d)")
    y_rows = out_0.rearrange("b s r d -> (b s) (r d)")
    pw = out_1.rearrange("a p m t -> (a p) (m t)").bitcast(I32)
    psc = out_2.rearrange("a q m -> (a q) m").bitcast(I32)

    with ExitStack() as ctx:
        keep = ctx.enter_context(tc.tile_pool(name="keep", bufs=1))
        big = ctx.enter_context(tc.tile_pool(name="big", bufs=2))
        prod = ctx.enter_context(tc.tile_pool(name="prod", bufs=3))
        small = ctx.enter_context(tc.tile_pool(name="small", bufs=2))
        psum = ctx.enter_context(tc.psum_pool(name="psum", bufs=2))

        warm = keep.tile([P, 1], F32, name="warm")
        nc.vector.memset(warm[:], 0.0)
        nc.scalar.activation(out=warm[:], in_=warm[:], func=ACT.Exp)
        ident = keep.tile([P, P], F32, name="ident")
        make_identity(nc, ident[:])
        x_tiles = []
        for k in range(NT):
            xs = keep.tile([P, R * D], BF16, name="xs%d" % k, align_bytes=64)
            x_tiles.append(xs)
        nc.sync.dma_start(out=x_tiles[0][:], in_=x_rows[0:P, :])
        gn_t = keep.tile([P, R, 4], BF16, name="gn_t")
        nc.sync.dma_start(out=gn_t[:], in_=gn.rearrange("(r p t) -> p r t", r=R, t=4))
        phi_w = keep.tile([P, 4, 2 * M], U8, name="phi_w", align_bytes=64)
        nc.sync.dma_start(out=phi_w[:].bitcast(I32), in_=phi_words.bitcast(I32).rearrange("g p b -> p g b"))
        phi_s = keep.tile([P, 4, M], U8, name="phi_s", align_bytes=64)
        nc.vector.memset(phi_s[:].bitcast(I32), 0)
        phi_sc32 = phi_scales.bitcast(I32)
        for q in range(4):
            nc.sync.dma_start(
                out=phi_s[32 * q : 32 * q + 4, :, :].bitcast(I32),
                in_=phi_sc32[:, 4 * q : 4 * q + 4, :].rearrange("g q n -> q g n"),
            )
        bm_t = keep.tile([P, M], BF16, name="bm_t")
        nc.sync.dma_start(out=bm_t[:], in_=bm.partition_broadcast(P))
        nc.sync.dma_start(out=x_tiles[1][:], in_=x_rows[P : 2 * P, :])
        gf_t = keep.tile([P, 4], BF16, name="gf_t")
        nc.sync.dma_start(out=gf_t[:], in_=gf.rearrange("(p t) -> p t", t=4))
        w_raw = keep.tile([P, 2 * D], U8, name="w_raw", align_bytes=64)
        nc.sync.dma_start(out=w_raw[:].bitcast(I32), in_=w_words.rearrange("a p b -> (a p) b").bitcast(I32))
        ws_raw = keep.tile([P, D], U8, name="ws_raw", align_bytes=64)
        nc.vector.memset(ws_raw[:].bitcast(I32), 0)
        w_sc32 = w_scales.rearrange("a q n -> (a q) n").bitcast(I32)
        for q in range(4):
            nc.sync.dma_start(out=ws_raw[32 * q : 32 * q + 4, :].bitcast(I32), in_=w_sc32[4 * q : 4 * q + 4, :])
        w_t = keep.tile([P, 4, P, 2], U8, name="w_t", align_bytes=64)
        nc.vector.tensor_copy(out=w_t[:], in_=w_raw[:].rearrange("p (m t b) -> p t m b", t=4, b=2))
        ws_t = keep.tile([P, 4, P], U8, name="ws_t", align_bytes=64)
        nc.vector.tensor_copy(out=ws_t[:], in_=ws_raw[:].rearrange("p (m t) -> p t m", t=4))
        w_flat = w_t[:].rearrange("p t m b -> p (t m b)")
        ws_flat = ws_t[:].rearrange("p t m -> p (t m)")
        pl_s = keep.tile([P, TOKENS * R], U8, name="pl_s", align_bytes=64)

        for k in range(2, NT):
            nc.sync.dma_start(out=x_tiles[k][:], in_=x_rows[k * P : (k + 1) * P, :])

        xt_t, xc_t, xs_t, tl_t, th_t, pre_t, qc_t, up_t, ut_t, ug_t, uc_t, us_t = ({} for i in range(12))
        ht_t, rl_t, f_t, mx_t, q_t, s_t, pr_t, a_t, c_t, b_t, qe_t, pb_t = ({} for i in range(12))
        post_t, fp_t, cb_t, pm_t, yp_t, y_t, yb_t, yt_t, bank_t, xn_t, tp_t = ({} for i in range(11))

        def x_words(k, h):
            words = x_tiles[k][:].bitcast(F32)
            bank = psum.tile([P, 4, P], F32, name="xw", tag="xw")
            bank_t[k, h] = bank
            for a in range(2):
                for u in range(2):
                    r = 2 * h + a
                    nc.tensor.transpose(bank[:, 2 * a + u, :], words[:, 256 * r + u : 256 * (r + 1) : 2], ident[:])

        def x_copy(k, h):
            if h == 0:
                xt = big.tile([P, R, P, 4], BF16, name="xt", bufs=5, align_bytes=64)
                xt_t[k] = xt
            xt_w = xt_t[k][:].rearrange("p r n t -> p (r n t)").bitcast(F32)
            nc.scalar.copy(
                out=xt_w[:, h * 512 : (h + 1) * 512].rearrange("p (a n u) -> p a n u", a=2, u=2),
                in_=bank_t[k, h][:].rearrange("p (a u) n -> p a n u", u=2),
            )

        def x_gain(k):
            xn = big.tile([P, R, P, 4], BF16, name="xn", align_bytes=64)
            xn_t[k] = xn
            nc.vector.tensor_mul(xn[:], xt_t[k][:], bc(gn_t[:], 2, P))

        def x_quant(k):
            xc = big.tile([P, R * P], U32, name="xc", align_bytes=64)
            xsc = big.tile([P, R * P], U8, name="xsc", align_bytes=64)
            xc_t[k], xs_t[k] = xc, xsc
            nc.vector.quantize_mx(out=xc[:].bitcast(FP8X4), scales=xsc[:], in_=xn_t[k][:].rearrange("p r n t -> p (r n t)"))

        def mx_one(k):
            tp = psum.tile([P, 512], F32, name="tp", tag="s")
            tp_t[k] = tp
            for n in range(3):
                for r in range(R):
                    nc.tensor.matmul_mx(
                        out=tp[:, n * P : (n + 1) * P],
                        lhsT=xc_t[k][:, r * P : (r + 1) * P].bitcast(FP8X4),
                        lhsT_scale=xs_t[k][:, r * P : (r + 1) * P],
                        rhs=phi_w[:, r, 256 * n : 256 * (n + 1)].bitcast(FP4X4),
                        rhs_scale=phi_s[:, r, n * P : (n + 1) * P],
                        start=(r == 0),
                        stop=(r == R - 1),
                    )

        def t_bias(k):
            tl = small.tile([P, K, G], F32, name="tl")
            tl_t[k] = tl
            nc.vector.tensor_add(
                tl[:],
                tp_t[k][:, :M].rearrange("p (g k) -> p k g", g=G),
                bm_t[:].rearrange("p (g k) -> p k g", g=G),
            )

        def tanh(k):
            th = small.tile([P, 8, G], F32, name="th")
            th_t[k] = th
            nc.scalar.activation(out=th[:], in_=tl_t[k][:, 0:8, :], func=ACT.Tanh, scale=0.5)

        def pre_post(k):
            pre = small.tile([P, 4, G], F32, name="pre")
            pre_t[k] = pre
            nc.vector.tensor_scalar(out=pre[:], in0=th_t[k][:, 0:4, :], scalar1=0.5, scalar2=0.5, op0=ALU.mult, op1=ALU.add)
            qc = small.tile([P, 20, G], F32, name="qc", bufs=3)
            qc_t[k] = qc
            nc.vector.tensor_scalar_add(qc[:, 16:20, :], th_t[k][:, 4:8, :], 1.0)

        def u_prod(k, r):
            if r == 0:
                up = big.tile([P, R, 4, P], F32, name="up")
                up_t[k] = up
            nc.gpsimd.tensor_mul(
                up_t[k][:, r, :, :].rearrange("p t (g e) -> p t g e", e=8),
                x_tiles[k][:, r * D : (r + 1) * D].rearrange("p (g e t) -> p t g e", e=8, t=4),
                bc(bc(pre_t[k][:, r, :], 1, 4), 3, 8),
            )

        def u_sum(k):
            ut = psum.tile([P, 4, P], F32, name="ut", tag="s")
            ut_t[k] = ut
            for t in range(4):
                for r in range(R):
                    nc.tensor.matmul(
                        out=ut[:, t, :], lhsT=up_t[k][:, r, t, :], rhs=ident[:], is_transpose=True, start=(r == 0), stop=(r == R - 1)
                    )

        def u_gain(k):
            ug = small.tile([P, P, 4], BF16, name="ug", align_bytes=64)
            ug_t[k] = ug
            nc.vector.tensor_mul(ug[:], ut_t[k][:].rearrange("p t n -> p n t"), bc(gf_t[:], 1, P))

        def u_quant(k):
            uc = small.tile([P, P], U32, name="uc", align_bytes=64)
            usc = small.tile([P, P], U8, name="usc", align_bytes=64)
            uc_t[k], us_t[k] = uc, usc
            nc.vector.quantize_mx(out=uc[:].bitcast(FP8X4), scales=usc[:], in_=ug_t[k][:].rearrange("p n t -> p (n t)"))

        def mx_two(k):
            ht = psum.tile([P, 4, P], F32, name="ht", tag="s")
            ht_t[k] = ht
            for t in range(4):
                nc.tensor.matmul_mx(
                    out=ht[:, t, :],
                    lhsT=w_flat[:, 256 * t : 256 * (t + 1)].bitcast(FP4X4),
                    lhsT_scale=ws_flat[:, P * t : P * (t + 1)],
                    rhs=uc_t[k][:].bitcast(FP8X4),
                    rhs_scale=us_t[k][:],
                    start=True,
                    stop=True,
                )

        def relu(k):
            rl = small.tile([P, 4, P], F32, name="rl")
            rl_t[k] = rl
            nc.scalar.activation(out=rl[:], in_=ht_t[k][:], func=ACT.Relu)

        def square(k):
            f = small.tile([P, 4, P], F32, name="f")
            f_t[k] = f
            nc.scalar.activation(out=f[:], in_=rl_t[k][:], func=ACT.Square)

        def row_max(k):
            mx = small.tile([P, 4, G], F32, name="mx")
            mx_t[k] = mx
            nc.vector.tensor_reduce(
                out=mx[:], in_=tl_t[k][:, 8:24, :].rearrange("p (i j) g -> p i g j", j=4), axis=AX.X, op=ALU.max
            )

        def sub_max(k):
            l = small.tile([P, 4, 4, G], F32, name="l")
            q_t[k] = l
            nc.gpsimd.tensor_sub(l[:], tl_t[k][:, 8:24, :].rearrange("p (i j) g -> p i j g", j=4), bc(mx_t[k][:], 2, 4))

        def exp(k):
            q = small.tile([P, 4, 4, G], F32, name="q0")
            nc.scalar.activation(out=q[:], in_=q_t[k][:], func=ACT.Exp)
            q_t[k] = q

        def row_sum(k, rnd):
            s = small.tile([P, 4, G], F32, name="s%d" % rnd)
            s_t[k] = s[:].rearrange("p (h e) g -> p h e g", e=2)
            nc.vector.tensor_reduce(out=s[:], in_=q_t[k][:].rearrange("p i j g -> p i g j"), axis=AX.X, op=ALU.add)

        def row_pair(k, rnd):
            pr = small.tile([P, 2, G], F32, name="pr%d" % rnd)
            pr_t[k] = pr
            nc.vector.tensor_mul(pr[:], s_t[k][:, :, 0, :], s_t[k][:, :, 1, :])

        def row_scale(k, rnd):
            a = small.tile([P, 2, 2, G], F32, name="a%d" % rnd)
            a_t[k] = a
            nc.vector.tensor_mul(a[:], s_t[k][:, :, ::-1, :], bc(pr_t[k][:, ::-1, :], 2, 2))

        def row_mul(k, rnd):
            q1 = small.tile([P, 4, 4, G], F32, name="qa%d" % rnd)
            nc.gpsimd.tensor_mul(q1[:], q_t[k][:], bc(a_t[k][:].rearrange("p h e g -> p (h e) g"), 2, 4))
            q_t[k] = q1

        def col_sum(k, rnd):
            c = small.tile([P, 4 * G], F32, name="c%d" % rnd)
            c_t[k] = c
            nc.vector.tensor_reduce(out=c[:], in_=q_t[k][:].rearrange("p i j g -> p (j g) i"), axis=AX.X, op=ALU.add)

        def col_recip(k, rnd):
            b = small.tile([P, 4 * G], F32, name="b%d" % rnd)
            b_t[k] = b
            nc.vector.reciprocal(b[:], c_t[k][:])

        def col_mul(k, rnd):
            if rnd == 0:
                q = small.tile([P, 4, 4, G], F32, name="qb")
                dst = q[:].rearrange("p i j g -> p i (j g)")
            else:
                q = None
                dst = qc_t[k][:, 0:16, :].rearrange("p (i j) g -> p i (j g)", j=4)
            nc.gpsimd.tensor_mul(dst, q_t[k][:].rearrange("p i j g -> p i (j g)"), bc(b_t[k][:], 1, 4))
            q_t[k] = q

        def expand(k, i):
            if i == 4:
                qe = big.tile([P, 20, G, 8], F32, name="qe")
                qe_t[k] = qe
            sl = slice(4 * i, 4 * i + 4)
            nc.scalar.copy(
                out=qe_t[k][:, sl, :, :].rearrange("p k g e -> p (k g) e"),
                in_=bc(qc_t[k][:, sl, :].rearrange("p k g -> p (k g)"), 2, 8),
            )

        def coef(k, i, tag):
            qf = qe_t[k][:].rearrange("p k g e -> p k (g e)")
            cb = psum.tile([P, 4, P], F32, name="cb" + tag, tag=tag)
            cb_t[k, i] = cb
            for j in range(4):
                nc.tensor.transpose(cb[:, j, :], qf[:, 4 * i + j, :], ident[:])

        def post_copy(k):
            post = small.tile([P, 4, P], F32, name="post")
            post_t[k] = post
            nc.scalar.copy(out=post[:], in_=cb_t[k, 4][:])

        def f_prod(k, i):
            if i == 0:
                fp = big.tile([P, 4, 4, P], F32, name="fp")
                fp_t[k] = fp
            nc.gpsimd.tensor_mul(fp_t[k][:, i, :, :], f_t[k][:], bc(post_t[k][:, i, :], 1, 4))

        def product(k, i):
            pm = prod.tile([P, 4, 4, P], F32, name="pm")
            pm_t[k, i] = pm
            nc.vector.tensor_mul(pm[:], xt_t[k][:].rearrange("p j n t -> p j t n"), bc(cb_t[k, i][:], 2, 4))

        def y_sum(k, i):
            yp = psum.tile([P, 4, P], F32, name="yp", tag="y")
            yp_t[k, i] = yp
            for t in range(4):
                for j in range(4):
                    nc.tensor.matmul(
                        out=yp[:, t, :], lhsT=pm_t[k, i][:, j, t, :], rhs=ident[:], is_transpose=True, start=(j == 0), stop=False
                    )
                nc.tensor.matmul(out=yp[:, t, :], lhsT=fp_t[k][:, i, t, :], rhs=ident[:], is_transpose=True, start=False, stop=True)

        def y_copy(k, i):
            if i == 0:
                y = big.tile([P, 4, D], F32, name="y")
                yb = big.tile([P, 4, D], BF16, name="yb", align_bytes=64)
                y_t[k], yb_t[k] = y, yb
            nc.scalar.copy(
                out=y_t[k][:, i, :].rearrange("p (c t) -> p c t", t=4), in_=yp_t[k, i][:].rearrange("p t c -> p c t")
            )

        def y_cast(k, i):
            nc.scalar.copy(out=yb_t[k][:, i, :], in_=y_t[k][:, i, :])

        def y_store(k, h):
            nc.sync.dma_start(
                out=y_rows[k * P : (k + 1) * P, h * 1024 : (h + 1) * 1024],
                in_=y_t[k][:, 2 * h : 2 * h + 2, :].rearrange("p i d -> p (i d)"),
            )

        def y_words(k, h):
            yw = yb_t[k][:].rearrange("p i d -> p (i d)").bitcast(F32)
            bank = psum.tile([P, 4, P], F32, name="yw", tag="xw")
            bank_t[k, 2 + h] = bank
            for a in range(2):
                for u in range(2):
                    i = 2 * h + a
                    nc.tensor.transpose(bank[:, 2 * a + u, :], yw[:, 256 * i + u : 256 * (i + 1) : 2], ident[:])

        def yt_copy(k, h):
            if h == 0:
                yt = big.tile([P, P, 4, 4], BF16, name="yt", align_bytes=64)
                yt_t[k] = yt
            yt_w = yt_t[k][:].rearrange("p n i t -> p (n i t)").bitcast(F32).rearrange("p (n i u) -> p n i u", i=4, u=2)
            nc.scalar.copy(
                out=yt_w[:, :, 2 * h : 2 * h + 2, :], in_=bank_t[k, 2 + h][:].rearrange("p (a u) n -> p n a u", u=2)
            )

        def y_quant(k):
            pc = big.tile([P, 4 * P], U32, name="pc", align_bytes=64)
            nc.vector.quantize_mx(
                out=pc[:].bitcast(FP8X4),
                scales=pl_s[:, k * 512 : (k + 1) * 512],
                in_=yt_t[k][:].rearrange("p n i t -> p (n i t)"),
            )
            nc.sync.dma_start(out=pw[:, k * 512 : (k + 1) * 512], in_=pc[:].bitcast(I32))

        def step(n):
            r = n % 4

            def at(offset, fn, *args):
                if (n - offset) % 4 == 0 and 0 <= (n - offset) // 4 < NT:
                    fn((n - offset) // 4, *args)

            def each(offset, fn, *args):
                m = n - offset
                if 0 <= m < 4 * NT:
                    fn(m // 4, m % 4, *args)

            at(-8, pre_post)
            each(0, product)
            at(-7, exp)
            at(-1, square)
            each(2, y_copy)
            each(-2, expand)
            at(-3, expand, 4)
            at(-9, mx_one)
            at(-2, mx_two)
            each(-1, coef, "c")
            each(1, y_sum)
            at(-4, u_sum)
            at(-3, coef, 4, "s")
            at(-15, x_words, 0)
            at(-13, x_words, 1)
            at(4, y_words, 0)
            at(6, y_words, 1)
            at(-2, post_copy)
            at(-2, relu)
            each(2, y_cast)
            at(5, yt_copy, 0)
            at(7, yt_copy, 1)
            at(-14, x_copy, 0)
            at(-12, x_copy, 1)
            at(3, y_store, 0)
            at(5, y_store, 1)
            each(-1, f_prod)
            for i in range(4):
                at(-8 + i, u_prod, i)
            at(-9, t_bias)
            at(-7, row_sum, 0)
            at(-6, col_sum, 0)
            at(-5, row_sum, 1)
            at(-4, col_sum, 1)
            at(-9, tanh)
            at(-8, row_max)
            at(-11, x_gain)
            at(-10, x_quant)
            at(-7, row_pair, 0)
            at(-6, col_recip, 0)
            at(-5, row_pair, 1)
            at(-4, col_recip, 1)
            at(-8, sub_max)
            at(-4, u_gain)
            at(-3, u_quant)
            at(7, y_quant)
            at(-7, row_scale, 0)
            at(-5, row_scale, 1)
            at(-7, row_mul, 0)
            at(-6, col_mul, 0)
            at(-5, row_mul, 1)
            at(-4, col_mul, 1)

        with tc.manual_schedule():
            for n in range(-15, 4 * NT + 4):
                step(n)
        for q in range(4):
            nc.sync.dma_start(out=psc[4 * q : 4 * q + 4, :], in_=pl_s[32 * q : 32 * q + 4, :].bitcast(I32))
